import numpy as np
import ml_dtypes


def mxq(x, axis, fmt="e4m3"):
    dtype, down = {"e4m3": (ml_dtypes.float8_e4m3fn, 7), "e5m2": (ml_dtypes.float8_e5m2, 14)}[fmt]
    v = np.moveaxis(np.asarray(x, np.float32).astype(ml_dtypes.bfloat16).astype(np.float64), axis, -1)
    blocks = v.reshape(v.shape[:-1] + (-1, 32))
    amax = np.abs(blocks).max(-1, keepdims=True)
    byte = np.maximum(np.where(amax > 0, np.frexp(amax)[1] - 1 + 127, 0) - down, 1)
    scale = np.exp2(byte - 127.0)
    codes = (blocks / scale).astype(np.float32).astype(dtype).astype(np.float64)
    return np.moveaxis((codes * scale).reshape(v.shape), -1, axis)


WIDE = False


def mx_kscale(k):
    if not WIDE:
        return np.ones(k)
    levels = np.array([10, -10, 5, -5, 0])
    if k % 512:
        return np.exp2(np.random.permutation(np.resize(levels, k // 32))).repeat(32)
    a = np.empty((k // 512, 16))
    for p in range(k // 512):
        a[p, :8] = np.random.permutation(np.resize(levels, 8))
        for g in range(8):
            far = levels[np.abs(levels - a[p, g]) >= 10]
            a[p, g + 8] = far[np.random.randint(len(far))]
    return np.exp2(a.ravel()).repeat(32)


def f64(x):
    return np.asarray(x).astype(np.float64)


def striped(idx):
    return np.tile(np.asarray(idx).reshape(-1, 16).T, (8, 1)).astype(np.uint16)


def unstriped(offs):
    return offs[:16].T.reshape(-1).astype(np.int64)


E2M1 = np.array([0.0, 0.5, 1.0, 1.5, 2.0, 3.0, 4.0, 6.0, -0.0, -0.5, -1.0, -1.5, -2.0, -3.0, -4.0, -6.0])


def pack_weight(w, fmt):
    k, n = w.shape
    w = f64(np.asarray(w, np.float32).astype(ml_dtypes.bfloat16)).reshape(k // 32, 32, n)
    amax = np.abs(w).max(1)
    if fmt == "e4m3":
        byte = np.frexp(amax)[1] - 1 + 127 - 7
    else:
        mant, ex = np.frexp(amax / 6.0)
        byte = np.where(mant > 0.5, ex, ex - 1) + 127
    byte = np.clip(np.where(amax > 0, byte, 1), 1, 254)
    scaled = (w * np.exp2(127.0 - byte)[:, None, :]).reshape(k, n).astype(np.float32)
    by_word = np.ascontiguousarray(scaled.reshape(k // 512, 128, 4, n).transpose(0, 1, 3, 2))
    if fmt == "e4m3":
        words = by_word.astype(ml_dtypes.float8_e4m3fn).view(np.uint8)
    else:
        c = by_word.astype(ml_dtypes.float4_e2m1fn).view(np.uint8) & 0xF
        words = (c[..., 0::2] | (c[..., 1::2] << 4)).reshape(k // 512, 128, 2 * n)
    return np.ascontiguousarray(words), np.ascontiguousarray(byte.astype(np.uint8).reshape(k // 512, 16, n))


def unpack_weight(words, scales, fmt):
    g, _, n = scales.shape
    words = np.ascontiguousarray(words).reshape(g, 128, n, -1)
    if fmt == "e4m3":
        vals = words.view(ml_dtypes.float8_e4m3fn).astype(np.float64)
    else:
        nib = np.empty((g, 128, n, 4), np.uint8)
        nib[..., 0::2] = words & 0xF
        nib[..., 1::2] = words >> 4
        vals = E2M1[nib]
    vals = vals * np.repeat(np.exp2(scales.astype(np.float64) - 127.0), 8, axis=1)[..., None]
    return vals.transpose(0, 1, 3, 2).reshape(g * 512, n)


def sigmoid(v):
    return 1.0 / (1.0 + np.exp(-v))


D, E, T, I, Q, G = 512, 512, 2048, 512, 128, 64


def setup_inputs():
    n = np.random.standard_normal
    idx = np.random.permutation(T)[:I]
    fd = mx_kscale(D)
    fe = mx_kscale(E)
    fi = mx_kscale(I)
    ti = np.ones(T)
    ti[idx] = fi
    keysp = pack_weight(n((D, T)) / fd[:, None], "e2m1")
    valsp = pack_weight(n((E, T)) / fe[:, None], "e2m1")
    return {
        "query": (n((D, Q)) * 0.6 / np.sqrt(D) * fd[:, None]).astype(np.float32),
        "keys_words": keysp[0],
        "keys_scales": keysp[1],
        "gout": (n((E, Q)) * 1 / np.sqrt(E) * fe[:, None]).astype(np.float32),
        "vals_words": valsp[0],
        "vals_scales": valsp[1],
        "size": (np.random.uniform(0.1, 0.4, (1, I))).astype(np.float32),
        "dquery": (n((D, Q)) * 1.0 / np.sqrt(D) * fd[:, None]).astype(np.float32),
        "fs": (np.random.uniform(128.0, 512.0, (1, I)) * fi).astype(np.float32),
        "keyrows": (n((D, T)) / ti).astype(np.float32),
        "res": (n((Q, D)) * 4.0).astype(np.float32),
        "offs": striped(idx),
    }


def reference(query, keys_words, keys_scales, gout, vals_words, vals_scales, size, dquery, fs, keyrows, res, offs):
    idx = unstriped(offs)
    keysu = unpack_weight(keys_words, keys_scales, "e2m1")
    valsu = unpack_weight(vals_words, vals_scales, "e2m1")
    queryq = mxq(f64(query), 0, "e4m3")
    keysidxg = keysu[:, idx]
    a = queryq.T @ keysidxg
    dqueryq = mxq(f64(dquery), 0, "e4m3")
    ta = dqueryq.T @ keysidxg
    s = a.reshape(Q, G, I // G).mean(axis=2)
    p = np.exp(s - np.max(s, axis=1, keepdims=True))
    z = np.sum(p, axis=1, keepdims=True)
    r = p / z
    rr = np.repeat(r, I // G, axis=1)
    goutq = mxq(f64(gout), 0, "e4m3")
    valsidxg = valsu[:, idx]
    c0 = goutq.T @ valsidxg
    drr = c0 * f64(size) * sigmoid(a)
    dr = drr.reshape(Q, G, I // G).sum(axis=2)
    dz = np.sum(dr * p / np.square(z) * (-1.0), axis=1, keepdims=True)
    dp = dr / z + dz
    ts = ta.reshape(Q, G, I // G).mean(axis=2)
    tp = ts * p
    tz = np.sum(tp, axis=1, keepdims=True)
    tr = (tp - tz * p / z) / z
    trr = np.repeat(tr, I // G, axis=1)
    tdrr = ta * sigmoid(a) * (1.0 - sigmoid(a)) * c0 * f64(size)
    tdr = tdrr.reshape(Q, G, I // G).sum(axis=2)
    tdz = np.sum((tdr * p + tp * dr - tz * z * 2.0 * dr * p / np.square(z)) / np.square(z) * (-1.0), axis=1, keepdims=True)
    tdp = (tdr - tz * dr / z) / z + tdz
    tds = tdp * p + tp * dp
    te1 = tds / 8.0
    tr1 = np.repeat(te1, I // G, axis=1)
    tda = (trr * c0 * f64(size) * sigmoid(a) + ta * sigmoid(a) * (1.0 - sigmoid(a)) * c0 * f64(size) * rr) * (1.0 - sigmoid(a)) + ta * sigmoid(a) * (1.0 - sigmoid(a)) * (-1.0) * c0 * f64(size) * rr * sigmoid(a) + tr1
    gs = tda * f64(fs)
    gt1 = gs.T
    kt = f64(keyrows)[:, idx].T
    gt1q = mxq(gt1, 0, "e4m3")
    ktq = mxq(kt, 0, "e4m3")
    gq = gt1q.T @ ktq
    y = gq + f64(res)
    return y

@@ -1,0 +1,259 @@
+from contextlib import ExitStack
+
+import concourse.mybir as mybir
+from concourse.masks import make_identity
+
+F32 = mybir.dt.float32
+BF16 = mybir.dt.bfloat16
+I32 = mybir.dt.int32
+U32 = mybir.dt.uint32
+U16 = mybir.dt.uint16
+U8 = mybir.dt.uint8
+FP8X4 = mybir.dt.float8_e4m3fn_x4
+FP4X4 = mybir.dt.float4_e2m1fn_x4
+ALU = mybir.AluOpType
+ACT = mybir.ActivationFunctionType
+AX = mybir.AxisListType
+
+P = 128
+POOL = 2048
+SLOTS = 512
+SPANS = 64
+SPAN = 8
+PACK = 4
+D = 512
+SCALAR_PLANES = 2
+FLOPS = 4 * 2 * 128 * 512 * 512
+
+
+def tile_attend_hvspanread_q_kernel(tc, query, keys_words, keys_scales, gout, vals_words, vals_scales,
+                                     size, dquery, fs, keyrows, res, offs, out):
+    nc = tc.nc
+    with ExitStack() as ctx:
+        sb = ctx.enter_context(tc.tile_pool(name="sb", bufs=1))
+        ps = ctx.enter_context(tc.psum_pool(name="ps", bufs=1))
+
+        def tile(name, shape, dtype, tag=None):
+            return sb.tile(shape, dtype, name=name, tag=tag or name, align_bytes=64)
+
+        offsets = sb.tile([P, SLOTS // 16], U16, name="offsets")
+        nc.sync.dma_start(offsets[:], offs)
+
+        def load_words(name, words):
+            t = tile(name, [P, POOL], U16)
+            nc.sync.dma_start(t[:].bitcast(I32), words[0].bitcast(I32))
+            return t
+
+        def load_scales(name, scales, queue):
+            t = tile(name, [P, POOL], U8)
+            for quad in range(4):
+                rows = scales[0, 4 * quad:4 * quad + 4, :].bitcast(I32).rearrange("(o r) c -> o r c", o=1)
+                queue.dma_start(t[32 * quad:32 * quad + 32, :].bitcast(I32), rows.to_broadcast([8, 4, POOL // 4]))
+            return t
+
+        def load_rows(name, rows):
+            t = tile(name, [P, PACK, P], F32)
+            nc.sync.dma_start(t[:], rows.rearrange("(p t) q -> p t q", t=PACK))
+            return t
+
+        def load_by_slot(name, row, queue):
+            t = tile(name, [P, PACK], F32)
+            queue.dma_start(t[:], row.rearrange("o (p t) -> (o p) t", t=PACK))
+            return t
+
+        k_scales = load_scales("k_scales", keys_scales, nc.sync)
+        k_words = load_words("k_words", keys_words)
+        q_raw = load_rows("q_raw", query)
+        dq_raw = load_rows("dq_raw", dquery)
+        v_scales = load_scales("v_scales", vals_scales, nc.sync)
+        size_pt = load_by_slot("size_pt", size, nc.gpsimd)
+        fs_pt = load_by_slot("fs_pt", fs, nc.gpsimd)
+        ident = tile("ident", [P, P], F32)
+        make_identity(nc, ident[:])
+        go_raw = load_rows("go_raw", gout)
+        v_words = load_words("v_words", vals_words)
+        planes = []
+        for b in range(D // P):
+            t = tile("plane%d" % b, [P, POOL], F32)
+            nc.sync.dma_start(t[:], keyrows[b * P:(b + 1) * P, :])
+            planes.append(t)
+        res_sb = tile("res_sb", [P, D], F32)
+        nc.sync.dma_start(res_sb[:], res)
+
+        def gather(name, window, dtype, tag=None):
+            t = tile(name, [P, SLOTS], dtype, tag)
+            nc.vector.tensor_copy(t[:], window[:].indirect(offsets[:]))
+            return t
+
+        def interleave(dst, raw):
+            nc.scalar.copy(out=dst.rearrange("p (c i t) -> p c t i", i=4, t=PACK),
+                           in_=raw[:].rearrange("p t (c i) -> p c t i", i=4))
+
+        ks_g = gather("ks_g", k_scales, U8)
+        kw_g = gather("kw_g", k_words, U16)
+        qd_bf = tile("qd_bf", [P, 2 * PACK * P], BF16)
+        interleave(qd_bf[:, 0:PACK * P], q_raw)
+        interleave(qd_bf[:, PACK * P:2 * PACK * P], dq_raw)
+        qd_codes = tile("qd_codes", [P, 2 * P], U32)
+        qd_scales = tile("qd_scales", [P, 2 * P], U8)
+        nc.vector.quantize_mx(out=qd_codes[:].bitcast(FP8X4), scales=qd_scales[:], in_=qd_bf[:])
+        a_ps = ps.tile([P, SLOTS], F32, name="a_ps", tag="a_gq")
+        ta_ps = ps.tile([P, SLOTS], F32, name="ta_ps", tag="ta")
+        for half, bank in enumerate((a_ps, ta_ps)):
+            cols = slice(half * P, (half + 1) * P)
+            nc.tensor.matmul_mx(out=bank[:], lhsT=qd_codes[:, cols].bitcast(FP8X4), lhsT_scale=qd_scales[:, cols],
+                                rhs=kw_g[:].bitcast(FP4X4), rhs_scale=ks_g[:], start=True, stop=True)
+
+        def by_place(bank):
+            return bank[:].rearrange("q (g j) -> q j g", j=SPAN)
+
+        th = tile("th", [P, SPAN, SPANS], F32)
+        nc.scalar.activation(out=th[:], in_=by_place(a_ps), func=ACT.Tanh, scale=0.5)
+        scores = tile("scores", [P, SPAN, 2 * SPANS], F32)
+        nc.scalar.copy(out=scores[:, :, 0:SPANS], in_=by_place(a_ps))
+        nc.scalar.copy(out=scores[:, :, SPANS:2 * SPANS], in_=by_place(ta_ps))
+
+        size_ps = ps.tile([P, PACK, P], F32, name="size_ps", tag="size_gs")
+        for t in range(PACK):
+            nc.tensor.transpose(size_ps[:, t, :], size_pt[:, t:t + 1].to_broadcast([P, P]), ident[:])
+        half_size = tile("half_size", [P, SPAN, SPANS], F32)
+        nc.scalar.activation(out=half_size[:].rearrange("q (h t) g -> q h t g", h=2),
+                             in_=size_ps[:].rearrange("q t (g h) -> q h t g", h=2), func=ACT.Copy, scale=0.5)
+
+        vs_g = gather("vs_g", v_scales, U8)
+        go_bf = tile("go_bf", [P, PACK * P], BF16)
+        interleave(go_bf[:], go_raw)
+        go_codes = tile("go_codes", [P, P], U32)
+        go_scales = tile("go_scales", [P, P], U8)
+        nc.vector.quantize_mx(out=go_codes[:].bitcast(FP8X4), scales=go_scales[:], in_=go_bf[:])
+        vw_g = tile("vw_g", [P, SLOTS], U16)
+        c0_halves = []
+        for half in range(2):
+            cols = slice(half * SLOTS // 2, (half + 1) * SLOTS // 2)
+            nc.vector.tensor_copy(vw_g[:, cols], v_words[:].indirect(offsets[:, half * 16:(half + 1) * 16]))
+            bank = ps.tile([P, SLOTS // 2], F32, name="c0_%d" % half, tag="xt", bufs=2)
+            nc.tensor.matmul_mx(out=bank[:], lhsT=go_codes[:].bitcast(FP8X4), lhsT_scale=go_scales[:],
+                                rhs=vw_g[:, cols].bitcast(FP4X4), rhs_scale=vs_g[:, cols], start=True, stop=True)
+            c0_halves.append(bank)
+
+        def span_sums(name, src, factor):
+            turned = ps.tile([P, P], F32, name=name + "_t", tag="turned")
+            for j in range(SPAN):
+                nc.tensor.matmul(turned[:], lhsT=src[:, j, :], rhs=ident[:], is_transpose=True,
+                                 start=(j == 0), stop=(j == SPAN - 1))
+            staged = tile(name + "_s", [P, P], F32)
+            nc.scalar.activation(out=staged[:], in_=turned[:], func=ACT.Copy, scale=factor)
+            back = ps.tile([P, P], F32, name=name, tag="back")
+            nc.tensor.transpose(back[:], staged[:], ident[:])
+            return back
+
+        means = span_sums("means", scores, 1.0 / SPAN)
+
+        cs = tile("cs", [P, SPAN, SPANS], F32)
+        for half, bank in enumerate(c0_halves):
+            spans = slice(half * SPANS // 2, (half + 1) * SPANS // 2)
+            nc.vector.tensor_tensor(out=cs[:, :, spans], in0=by_place(bank), in1=half_size[:, :, spans], op=ALU.mult)
+        grads = tile("grads", [P, SPAN, 2 * SPANS], F32)
+        drr = grads[:, :, 0:SPANS]
+        tdrr = grads[:, :, SPANS:2 * SPANS]
+        nc.vector.scalar_tensor_tensor(out=drr, in0=th[:], scalar=1.0, in1=cs[:], op0=ALU.add, op1=ALU.mult)
+        a_n = tile("a_n", [P, SPAN, SPANS], F32)
+        nc.vector.scalar_tensor_tensor(out=a_n[:], in0=th[:], scalar=1.0, in1=drr, op0=ALU.subtract, op1=ALU.mult)
+        nc.vector.scalar_tensor_tensor(out=tdrr, in0=a_n[:], scalar=-0.5, in1=scores[:, :, SPANS:2 * SPANS],
+                                       op0=ALU.mult, op1=ALU.mult)
+        neg_max = tile("neg_max", [P, 1], F32, "scores")
+        nc.vector.tensor_reduce(out=neg_max[:], in_=means[:, 0:SPANS], axis=AX.X, op=ALU.max, negate=True)
+        p_sb = tile("p_sb", [P, SPANS], F32)
+        z = tile("z", [P, 1], F32)
+        nc.scalar.activation(out=p_sb[:], in_=means[:, 0:SPANS], func=ACT.Exp, bias=neg_max[:], accum_out=z[:])
+        sums = span_sums("sums", grads, 0.25)
+
+        rz = tile("rz", [P, 1], F32)
+        nc.vector.reciprocal(out=rz[:], in_=z[:])
+        shares = tile("shares", [P, 2 * SPANS], F32)
+        tr = shares[:, 0:SPANS]
+        r = shares[:, SPANS:2 * SPANS]
+        mu = tile("mu", [P, 1], F32)
+        r_ts = tile("r_ts", [P, SPANS], F32)
+        nc.vector.scalar_tensor_tensor(out=r_ts[:], in0=p_sb[:], scalar=rz[:], in1=means[:, SPANS:2 * SPANS],
+                                       op0=ALU.mult, op1=ALU.mult, accum_out=mu[:])
+        nc.vector.tensor_scalar(out=r, in0=p_sb[:], scalar1=rz[:], scalar2=None, op0=ALU.mult)
+        nc.vector.scalar_tensor_tensor(out=tr, in0=means[:, SPANS:2 * SPANS], scalar=mu[:], in1=r,
+                                       op0=ALU.subtract, op1=ALU.mult)
+
+        b_2 = tile("b_2", [P, SPAN, SPANS], F32)
+        nc.vector.scalar_tensor_tensor(out=b_2[:], in0=th[:], scalar=2.0, in1=tdrr, op0=ALU.mult, op1=ALU.mult)
+
+        def spread(x, places):
+            return x.rearrange("q (a g b) -> q a g b", a=1, b=1).to_broadcast([P, places, SPANS, 2])
+
+        terms = []
+        for name, slotwise, spanwise in (("term_a", a_n, tr), ("term_b", b_2, r)):
+            t = tile(name, [P, PACK, P], F32)
+            nc.vector.tensor_tensor(out=t[:].rearrange("q t (g h) -> q t g h", h=2),
+                                    in0=slotwise[:].rearrange("q (h t) g -> q t g h", h=2),
+                                    in1=spread(spanwise, PACK), op=ALU.mult)
+            terms.append(t)
+
+        zz = tile("zz", [P, 2 * SPANS], F32)
+        total = tile("total", [P, 1], F32)
+        nc.vector.scalar_tensor_tensor(out=zz[:], in0=sums[:], scalar=1.0, in1=shares[:],
+                                       op0=ALU.mult, op1=ALU.mult, accum_out=total[:])
+        r_dr = tile("r_dr", [P, SPANS], F32)
+        m = tile("m", [P, 1], F32)
+        nc.vector.scalar_tensor_tensor(out=r_dr[:], in0=sums[:, 0:SPANS], scalar=1.0, in1=r,
+                                       op0=ALU.mult, op1=ALU.mult, accum_out=m[:])
+        u1 = tile("u1", [P, SPANS], F32)
+        u2 = tile("u2", [P, SPANS], F32)
+        nc.vector.scalar_tensor_tensor(out=u2[:], in0=r, scalar=total[:], in1=zz[:, SPANS:2 * SPANS],
+                                       op0=ALU.mult, op1=ALU.subtract)
+        nc.vector.scalar_tensor_tensor(out=u1[:], in0=tr, scalar=m[:], in1=zz[:, 0:SPANS],
+                                       op0=ALU.mult, op1=ALU.subtract)
+        w_n = tile("w_n", [P, P], F32)
+
+        def twice(x):
+            return x[:].rearrange("q (g b) -> q g b", b=1).to_broadcast([P, SPANS, 2])
+
+        nc.vector.tensor_tensor(out=w_n[:].rearrange("q (g h) -> q g h", h=2), in0=twice(u1), in1=twice(u2), op=ALU.add)
+
+        kt_bf = tile("kt_bf", [P, D * PACK], BF16)
+        kt_codes = tile("kt_codes", [P, D], U32)
+        kt_scales = tile("kt_scales", [P, D], U8)
+        for b in range(D // P):
+            if b < SCALAR_PLANES:
+                narrow = tile("narrow%d" % b, [P, POOL], BF16)
+                for c in range(0, POOL, 512):
+                    nc.scalar.activation(out=narrow[:, c:c + 512], in_=planes[b][:, c:c + 512], func=ACT.Copy)
+                rows = tile("rows%d" % b, [P, SLOTS], BF16, ("scores", "grads")[b])
+                nc.scalar.activation(out=rows[:], in_=narrow[:].indirect(offsets[:]), func=ACT.Copy)
+            else:
+                rows = gather("rows%d" % b, planes[b], BF16, {2: "u1"}.get(b))
+            words = rows[:].bitcast(F32)
+            xt = ps.tile([P, 2, P], F32, name="xt%d" % b, tag="xt", bufs=2)
+            for u in range(2):
+                nc.tensor.transpose(xt[:, u, :], words[:, u:SLOTS // 2:2], ident[:])
+            block = kt_bf[:, b * P * PACK:(b + 1) * P * PACK]
+            nc.scalar.copy(out=block.bitcast(F32).rearrange("p (d u) -> p d u", u=2),
+                           in_=xt[:].rearrange("p u d -> p d u"))
+            nc.vector.quantize_mx(out=kt_codes[:, b * P:(b + 1) * P].bitcast(FP8X4),
+                                  scales=kt_scales[:, b * P:(b + 1) * P], in_=block)
+
+        gs_ps = ps.tile([P, PACK, P], F32, name="gs_ps", tag="size_gs")
+        sources = [terms[0][:, t, :] for t in range(PACK)] + [terms[1][:, t, :] for t in range(PACK)] + [w_n[:]] * PACK
+        for n, src in enumerate(sources):
+            nc.tensor.matmul(gs_ps[:, n % PACK, :], lhsT=src, rhs=ident[:], is_transpose=True,
+                             start=(n == 0), stop=(n == len(sources) - 1))
+        gs_bf = tile("gs_bf", [P, P, PACK], BF16, "plane3")
+        nc.vector.scalar_tensor_tensor(out=gs_bf[:], in0=gs_ps[:].rearrange("p t q -> p q t"), scalar=-0.5,
+                                       in1=fs_pt[:].rearrange("p (o t) -> p o t", o=1).to_broadcast([P, P, PACK]),
+                                       op0=ALU.mult, op1=ALU.mult)
+        gs_codes = tile("gs_codes", [P, P], U32)
+        gs_scales = tile("gs_scales", [P, P], U8)
+        nc.vector.quantize_mx(out=gs_codes[:].bitcast(FP8X4), scales=gs_scales[:],
+                              in_=gs_bf[:].rearrange("p q t -> p (q t)"))
+        gq_ps = ps.tile([P, D], F32, name="gq_ps", tag="a_gq")
+        nc.tensor.matmul_mx(out=gq_ps[:], lhsT=gs_codes[:].bitcast(FP8X4), lhsT_scale=gs_scales[:],
+                            rhs=kt_codes[:].bitcast(FP8X4), rhs_scale=kt_scales[:], start=True, stop=True)
+        y = tile("y", [P, D], F32)
+        nc.vector.tensor_tensor(out=y[:], in0=gq_ps[:], in1=res_sb[:], op=ALU.add)
+        nc.sync.dma_start(out, y[:])

@@ -56,8 +56,8 @@ def tile_attend_hvspanread_q_kernel(tc, query, keys_words, keys_scales, gout, va
             nc.sync.dma_start(t[:], rows.rearrange("(p t) q -> p t q", t=PACK))
             return t
 
-        def load_by_slot(name, row, queue):
-            t = tile(name, [P, PACK], F32)
+        def load_by_slot(name, row, queue, tag=None):
+            t = tile(name, [P, PACK], F32, tag)
             queue.dma_start(t[:], row.rearrange("o (p t) -> (o p) t", t=PACK))
             return t
 
@@ -65,20 +65,13 @@ def tile_attend_hvspanread_q_kernel(tc, query, keys_words, keys_scales, gout, va
         k_words = load_words("k_words", keys_words)
         q_raw = load_rows("q_raw", query)
         dq_raw = load_rows("dq_raw", dquery)
-        v_scales = load_scales("v_scales", vals_scales, nc.sync)
-        size_pt = load_by_slot("size_pt", size, nc.gpsimd)
-        fs_pt = load_by_slot("fs_pt", fs, nc.gpsimd)
+        v_scales = load_scales("v_scales", vals_scales, nc.gpsimd)
         ident = tile("ident", [P, P], F32)
-        make_identity(nc, ident[:])
+        nc.vector.memset(ident[:], 0.0)
+        make_identity(nc, ident[:], nomemset=True)
         go_raw = load_rows("go_raw", gout)
+        size_pt = load_by_slot("size_pt", size, nc.sync)
         v_words = load_words("v_words", vals_words)
-        planes = []
-        for b in range(D // P):
-            t = tile("plane%d" % b, [P, POOL], F32)
-            nc.sync.dma_start(t[:], keyrows[b * P:(b + 1) * P, :])
-            planes.append(t)
-        res_sb = tile("res_sb", [P, D], F32)
-        nc.sync.dma_start(res_sb[:], res)
 
         def gather(name, window, dtype, tag=None):
             t = tile(name, [P, SLOTS], dtype, tag)
@@ -120,7 +113,7 @@ def tile_attend_hvspanread_q_kernel(tc, query, keys_words, keys_scales, gout, va
         nc.scalar.activation(out=half_size[:].rearrange("q (h t) g -> q h t g", h=2),
                              in_=size_ps[:].rearrange("q t (g h) -> q h t g", h=2), func=ACT.Copy, scale=0.5)
 
-        vs_g = gather("vs_g", v_scales, U8)
+        vs_g = gather("vs_g", v_scales, U8, "qd_bf")
         go_bf = tile("go_bf", [P, PACK * P], BF16)
         interleave(go_bf[:], go_raw)
         go_codes = tile("go_codes", [P, P], U32)
@@ -131,36 +124,68 @@ def tile_attend_hvspanread_q_kernel(tc, query, keys_words, keys_scales, gout, va
         for half in range(2):
             cols = slice(half * SLOTS // 2, (half + 1) * SLOTS // 2)
             nc.vector.tensor_copy(vw_g[:, cols], v_words[:].indirect(offsets[:, half * 16:(half + 1) * 16]))
-            bank = ps.tile([P, SLOTS // 2], F32, name="c0_%d" % half, tag="xt", bufs=2)
+            bank = ps.tile([P, SLOTS // 2], F32, name="c0_%d" % half, tag="c0_%d" % half)
             nc.tensor.matmul_mx(out=bank[:], lhsT=go_codes[:].bitcast(FP8X4), lhsT_scale=go_scales[:],
                                 rhs=vw_g[:, cols].bitcast(FP4X4), rhs_scale=vs_g[:, cols], start=True, stop=True)
             c0_halves.append(bank)
 
+        planes = []
+        for b, tag in enumerate((None, "q_raw", "dq_raw", "go_raw")):
+            t = tile("plane%d" % b, [P, POOL], F32, tag)
+            nc.sync.dma_start(t[:], keyrows[b * P:(b + 1) * P, :])
+            planes.append(t)
+        fs_pt = load_by_slot("fs_pt", fs, nc.sync, "go_bf")
+
+        kt_bf = [tile("kt_bf%d" % half, [P, D // 2 * PACK], BF16) for half in range(2)]
+
+
+        def key_rows(b):
+            if b < SCALAR_PLANES:
+                narrow = tile("narrow%d" % b, [P, POOL], BF16, (None, "grads")[b])
+                for c in range(0, POOL, 512):
+                    nc.scalar.activation(out=narrow[:, c:c + 512], in_=planes[b][:, c:c + 512], func=ACT.Copy)
+                rows = tile("rows%d" % b, [P, SLOTS], BF16, ("scores", None)[b])
+                nc.scalar.activation(out=rows[:], in_=narrow[:].indirect(offsets[:]), func=ACT.Copy)
+            else:
+                rows = gather("rows%d" % b, planes[b], BF16, ("a_n", "u1")[b - SCALAR_PLANES])
+            words = rows[:].bitcast(F32)
+            xt = ps.tile([P, 2, P], F32, name="xt%d" % b, tag=("c0_0", "size_gs", "means", "turned")[b])
+            for u in range(2):
+                nc.tensor.transpose(xt[:, u, :], words[:, u:SLOTS // 2:2], ident[:])
+            block = kt_bf[b // 2][:, (b % 2) * P * PACK:(b % 2 + 1) * P * PACK]
+            nc.scalar.copy(out=block.bitcast(F32).rearrange("p (d u) -> p d u", u=2),
+                           in_=xt[:].rearrange("p u d -> p d u"))
+
         def span_sums(name, src, factor):
-            turned = ps.tile([P, P], F32, name=name + "_t", tag="turned")
+            turned = ps.tile([P, P], F32, name=name + "_t", tag="c0_1")
             for j in range(SPAN):
                 nc.tensor.matmul(turned[:], lhsT=src[:, j, :], rhs=ident[:], is_transpose=True,
                                  start=(j == 0), stop=(j == SPAN - 1))
             staged = tile(name + "_s", [P, P], F32)
             nc.scalar.activation(out=staged[:], in_=turned[:], func=ACT.Copy, scale=factor)
-            back = ps.tile([P, P], F32, name=name, tag="back")
+            back = ps.tile([P, P], F32, name=name, tag=name)
             nc.tensor.transpose(back[:], staged[:], ident[:])
             return back
 
         means = span_sums("means", scores, 1.0 / SPAN)
 
         cs = tile("cs", [P, SPAN, SPANS], F32)
-        for half, bank in enumerate(c0_halves):
-            spans = slice(half * SPANS // 2, (half + 1) * SPANS // 2)
-            nc.vector.tensor_tensor(out=cs[:, :, spans], in0=by_place(bank), in1=half_size[:, :, spans], op=ALU.mult)
         grads = tile("grads", [P, SPAN, 2 * SPANS], F32)
         drr = grads[:, :, 0:SPANS]
         tdrr = grads[:, :, SPANS:2 * SPANS]
-        nc.vector.scalar_tensor_tensor(out=drr, in0=th[:], scalar=1.0, in1=cs[:], op0=ALU.add, op1=ALU.mult)
+        ta = scores[:, :, SPANS:2 * SPANS]
         a_n = tile("a_n", [P, SPAN, SPANS], F32)
-        nc.vector.scalar_tensor_tensor(out=a_n[:], in0=th[:], scalar=1.0, in1=drr, op0=ALU.subtract, op1=ALU.mult)
-        nc.vector.scalar_tensor_tensor(out=tdrr, in0=a_n[:], scalar=-0.5, in1=scores[:, :, SPANS:2 * SPANS],
-                                       op0=ALU.mult, op1=ALU.mult)
+        b_2 = tile("b_2", [P, SPAN, SPANS], F32)
+        halves = [slice(0, SPANS // 2), slice(SPANS // 2, SPANS)]
+        for s, bank in zip(halves, c0_halves):
+            nc.vector.tensor_tensor(out=cs[:, :, s], in0=by_place(bank), in1=half_size[:, :, s], op=ALU.mult)
+        for dst, in0, scalar, op0, in1 in ((drr, th, 1.0, ALU.add, cs), (a_n, th, 1.0, ALU.subtract, drr),
+                                           (tdrr, a_n, -0.5, ALU.mult, ta)):
+            for s in halves:
+                nc.vector.scalar_tensor_tensor(out=dst[:, :, s], in0=in0[:, :, s], scalar=scalar, in1=in1[:, :, s],
+                                               op0=op0, op1=ALU.mult)
+        res_sb = tile("res_sb", [P, D], F32, "cs")
+        nc.sync.dma_start(res_sb[:], res)
         neg_max = tile("neg_max", [P, 1], F32, "scores")
         nc.vector.tensor_reduce(out=neg_max[:], in_=means[:, 0:SPANS], axis=AX.X, op=ALU.max, negate=True)
         p_sb = tile("p_sb", [P, SPANS], F32)
@@ -168,6 +193,7 @@ def tile_attend_hvspanread_q_kernel(tc, query, keys_words, keys_scales, gout, va
         nc.scalar.activation(out=p_sb[:], in_=means[:, 0:SPANS], func=ACT.Exp, bias=neg_max[:], accum_out=z[:])
         sums = span_sums("sums", grads, 0.25)
 
+        nc.vector.scalar_tensor_tensor(out=b_2[:], in0=th[:], scalar=2.0, in1=tdrr, op0=ALU.mult, op1=ALU.mult)
         rz = tile("rz", [P, 1], F32)
         nc.vector.reciprocal(out=rz[:], in_=z[:])
         shares = tile("shares", [P, 2 * SPANS], F32)
@@ -181,21 +207,21 @@ def tile_attend_hvspanread_q_kernel(tc, query, keys_words, keys_scales, gout, va
         nc.vector.scalar_tensor_tensor(out=tr, in0=means[:, SPANS:2 * SPANS], scalar=mu[:], in1=r,
                                        op0=ALU.subtract, op1=ALU.mult)
 
-        b_2 = tile("b_2", [P, SPAN, SPANS], F32)
-        nc.vector.scalar_tensor_tensor(out=b_2[:], in0=th[:], scalar=2.0, in1=tdrr, op0=ALU.mult, op1=ALU.mult)
-
         def spread(x, places):
             return x.rearrange("q (a g b) -> q a g b", a=1, b=1).to_broadcast([P, places, SPANS, 2])
 
         terms = []
-        for name, slotwise, spanwise in (("term_a", a_n, tr), ("term_b", b_2, r)):
+        for name, slotwise, spanwise in (("term_b", b_2, r), ("term_a", a_n, tr)):
             t = tile(name, [P, PACK, P], F32)
             nc.vector.tensor_tensor(out=t[:].rearrange("q t (g h) -> q t g h", h=2),
                                     in0=slotwise[:].rearrange("q (h t) g -> q t g h", h=2),
                                     in1=spread(spanwise, PACK), op=ALU.mult)
             terms.append(t)
 
-        zz = tile("zz", [P, 2 * SPANS], F32)
+        key_rows(0)
+        key_rows(2)
+
+        zz = tile("zz", [P, 2 * SPANS], F32, "dq_raw")
         total = tile("total", [P, 1], F32)
         nc.vector.scalar_tensor_tensor(out=zz[:], in0=sums[:], scalar=1.0, in1=shares[:],
                                        op0=ALU.mult, op1=ALU.mult, accum_out=total[:])
@@ -216,44 +242,31 @@ def tile_attend_hvspanread_q_kernel(tc, query, keys_words, keys_scales, gout, va
 
         nc.vector.tensor_tensor(out=w_n[:].rearrange("q (g h) -> q g h", h=2), in0=twice(u1), in1=twice(u2), op=ALU.add)
 
-        kt_bf = tile("kt_bf", [P, D * PACK], BF16)
-        kt_codes = tile("kt_codes", [P, D], U32)
-        kt_scales = tile("kt_scales", [P, D], U8)
-        for b in range(D // P):
-            if b < SCALAR_PLANES:
-                narrow = tile("narrow%d" % b, [P, POOL], BF16)
-                for c in range(0, POOL, 512):
-                    nc.scalar.activation(out=narrow[:, c:c + 512], in_=planes[b][:, c:c + 512], func=ACT.Copy)
-                rows = tile("rows%d" % b, [P, SLOTS], BF16, ("scores", "grads")[b])
-                nc.scalar.activation(out=rows[:], in_=narrow[:].indirect(offsets[:]), func=ACT.Copy)
-            else:
-                rows = gather("rows%d" % b, planes[b], BF16, {2: "u1"}.get(b))
-            words = rows[:].bitcast(F32)
-            xt = ps.tile([P, 2, P], F32, name="xt%d" % b, tag="xt", bufs=2)
-            for u in range(2):
-                nc.tensor.transpose(xt[:, u, :], words[:, u:SLOTS // 2:2], ident[:])
-            block = kt_bf[:, b * P * PACK:(b + 1) * P * PACK]
-            nc.scalar.copy(out=block.bitcast(F32).rearrange("p (d u) -> p d u", u=2),
-                           in_=xt[:].rearrange("p u d -> p d u"))
-            nc.vector.quantize_mx(out=kt_codes[:, b * P:(b + 1) * P].bitcast(FP8X4),
-                                  scales=kt_scales[:, b * P:(b + 1) * P], in_=block)
+        key_rows(3)
 
         gs_ps = ps.tile([P, PACK, P], F32, name="gs_ps", tag="size_gs")
         sources = [terms[0][:, t, :] for t in range(PACK)] + [terms[1][:, t, :] for t in range(PACK)] + [w_n[:]] * PACK
         for n, src in enumerate(sources):
             nc.tensor.matmul(gs_ps[:, n % PACK, :], lhsT=src, rhs=ident[:], is_transpose=True,
                              start=(n == 0), stop=(n == len(sources) - 1))
-        gs_bf = tile("gs_bf", [P, P, PACK], BF16, "plane3")
+        gs_bf = tile("gs_bf", [P, P, PACK], BF16, "go_raw")
         nc.vector.scalar_tensor_tensor(out=gs_bf[:], in0=gs_ps[:].rearrange("p t q -> p q t"), scalar=-0.5,
                                        in1=fs_pt[:].rearrange("p (o t) -> p o t", o=1).to_broadcast([P, P, PACK]),
                                        op0=ALU.mult, op1=ALU.mult)
+        key_rows(1)
         gs_codes = tile("gs_codes", [P, P], U32)
         gs_scales = tile("gs_scales", [P, P], U8)
         nc.vector.quantize_mx(out=gs_codes[:].bitcast(FP8X4), scales=gs_scales[:],
                               in_=gs_bf[:].rearrange("p q t -> p (q t)"))
-        gq_ps = ps.tile([P, D], F32, name="gq_ps", tag="a_gq")
-        nc.tensor.matmul_mx(out=gq_ps[:], lhsT=gs_codes[:].bitcast(FP8X4), lhsT_scale=gs_scales[:],
-                            rhs=kt_codes[:].bitcast(FP8X4), rhs_scale=kt_scales[:], start=True, stop=True)
         y = tile("y", [P, D], F32)
-        nc.vector.tensor_tensor(out=y[:], in0=gq_ps[:], in1=res_sb[:], op=ALU.add)
-        nc.sync.dma_start(out, y[:])
+        for half, tag in ((1, "a_gq"), (0, "ta")):
+            cols = slice(half * D // 2, (half + 1) * D // 2)
+            kt_codes = tile("kt_codes%d" % half, [P, D // 2], U32, ("u1", None)[half])
+            kt_scales = tile("kt_scales%d" % half, [P, D // 2], U8)
+            nc.vector.quantize_mx(out=kt_codes[:].bitcast(FP8X4), scales=kt_scales[:], in_=kt_bf[half][:])
+            gq_ps = ps.tile([P, D // 2], F32, name="gq%d" % half, tag=tag)
+            nc.tensor.matmul_mx(out=gq_ps[:], lhsT=gs_codes[:].bitcast(FP8X4), lhsT_scale=gs_scales[:],
+                                rhs=kt_codes[:].bitcast(FP8X4), rhs_scale=kt_scales[:],
+                                start=True, stop=True)
+            nc.vector.tensor_tensor(out=y[:, cols], in0=gq_ps[:], in1=res_sb[:, cols], op=ALU.add)
+            nc.sync.dma_start(out[:, cols], y[:, cols])

@@ -44,11 +44,11 @@ def tile_attend_hvspanread_q_kernel(tc, query, keys_words, keys_scales, gout, va
             nc.sync.dma_start(t[:].bitcast(I32), words[0].bitcast(I32))
             return t
 
-        def load_scales(name, scales, queue):
+        def load_scales(name, scales, clear):
             t = tile(name, [P, POOL], U8)
-            for quad in range(4):
-                rows = scales[0, 4 * quad:4 * quad + 4, :].bitcast(I32).rearrange("(o r) c -> o r c", o=1)
-                queue.dma_start(t[32 * quad:32 * quad + 32, :].bitcast(I32), rows.to_broadcast([8, 4, POOL // 4]))
+            clear.memset(t[:].bitcast(I32), 0)
+            for r in range(4):
+                nc.sync.dma_start(t[r:P:32, :].bitcast(I32), scales[0, r:16:4, :].bitcast(I32))
             return t
 
         def load_rows(name, rows):
@@ -61,14 +61,13 @@ def tile_attend_hvspanread_q_kernel(tc, query, keys_words, keys_scales, gout, va
             queue.dma_start(t[:], row.rearrange("o (p t) -> (o p) t", t=PACK))
             return t
 
-        k_scales = load_scales("k_scales", keys_scales, nc.sync)
         k_words = load_words("k_words", keys_words)
+        k_scales = load_scales("k_scales", keys_scales, nc.gpsimd)
         q_raw = load_rows("q_raw", query)
         dq_raw = load_rows("dq_raw", dquery)
-        v_scales = load_scales("v_scales", vals_scales, nc.gpsimd)
+        v_scales = load_scales("v_scales", vals_scales, nc.vector)
         ident = tile("ident", [P, P], F32)
-        nc.vector.memset(ident[:], 0.0)
-        make_identity(nc, ident[:], nomemset=True)
+        make_identity(nc, ident[:])
         go_raw = load_rows("go_raw", gout)
         size_pt = load_by_slot("size_pt", size, nc.sync)
         v_words = load_words("v_words", vals_words)
@@ -82,8 +81,8 @@ def tile_attend_hvspanread_q_kernel(tc, query, keys_words, keys_scales, gout, va
             nc.scalar.copy(out=dst.rearrange("p (c i t) -> p c t i", i=4, t=PACK),
                            in_=raw[:].rearrange("p t (c i) -> p c t i", i=4))
 
-        ks_g = gather("ks_g", k_scales, U8)
         kw_g = gather("kw_g", k_words, U16)
+        ks_g = gather("ks_g", k_scales, U8)
         qd_bf = tile("qd_bf", [P, 2 * PACK * P], BF16)
         interleave(qd_bf[:, 0:PACK * P], q_raw)
         interleave(qd_bf[:, PACK * P:2 * PACK * P], dq_raw)
@@ -130,11 +129,11 @@ def tile_attend_hvspanread_q_kernel(tc, query, keys_words, keys_scales, gout, va
             c0_halves.append(bank)
 
         planes = []
-        for b, tag in enumerate((None, "q_raw", "dq_raw", "go_raw")):
-            t = tile("plane%d" % b, [P, POOL], F32, tag)
+        for b in range(D // P):
+            t = tile("plane%d" % b, [P, POOL], F32)
             nc.sync.dma_start(t[:], keyrows[b * P:(b + 1) * P, :])
             planes.append(t)
-        fs_pt = load_by_slot("fs_pt", fs, nc.sync, "go_bf")
+        fs_pt = load_by_slot("fs_pt", fs, nc.sync)
 
         kt_bf = [tile("kt_bf%d" % half, [P, D // 2 * PACK], BF16) for half in range(2)]
 
@@ -144,12 +143,12 @@ def tile_attend_hvspanread_q_kernel(tc, query, keys_words, keys_scales, gout, va
                 narrow = tile("narrow%d" % b, [P, POOL], BF16, (None, "grads")[b])
                 for c in range(0, POOL, 512):
                     nc.scalar.activation(out=narrow[:, c:c + 512], in_=planes[b][:, c:c + 512], func=ACT.Copy)
-                rows = tile("rows%d" % b, [P, SLOTS], BF16, ("scores", None)[b])
+                rows = tile("rows%d" % b, [P, SLOTS], BF16, ("scores", "w_n")[b])
                 nc.scalar.activation(out=rows[:], in_=narrow[:].indirect(offsets[:]), func=ACT.Copy)
             else:
                 rows = gather("rows%d" % b, planes[b], BF16, ("a_n", "u1")[b - SCALAR_PLANES])
             words = rows[:].bitcast(F32)
-            xt = ps.tile([P, 2, P], F32, name="xt%d" % b, tag=("c0_0", "size_gs", "means", "turned")[b])
+            xt = ps.tile([P, 2, P], F32, name="xt%d" % b, tag=("c0_0", "means", "c0_1", "turned")[b])
             for u in range(2):
                 nc.tensor.transpose(xt[:, u, :], words[:, u:SLOTS // 2:2], ident[:])
             block = kt_bf[b // 2][:, (b % 2) * P * PACK:(b % 2 + 1) * P * PACK]
@@ -157,7 +156,7 @@ def tile_attend_hvspanread_q_kernel(tc, query, keys_words, keys_scales, gout, va
                            in_=xt[:].rearrange("p u d -> p d u"))
 
         def span_sums(name, src, factor):
-            turned = ps.tile([P, P], F32, name=name + "_t", tag="c0_1")
+            turned = ps.tile([P, P], F32, name=name + "_t", tag="turned")
             for j in range(SPAN):
                 nc.tensor.matmul(turned[:], lhsT=src[:, j, :], rhs=ident[:], is_transpose=True,
                                  start=(j == 0), stop=(j == SPAN - 1))
@@ -184,7 +183,7 @@ def tile_attend_hvspanread_q_kernel(tc, query, keys_words, keys_scales, gout, va
             for s in halves:
                 nc.vector.scalar_tensor_tensor(out=dst[:, :, s], in0=in0[:, :, s], scalar=scalar, in1=in1[:, :, s],
                                                op0=op0, op1=ALU.mult)
-        res_sb = tile("res_sb", [P, D], F32, "cs")
+        res_sb = tile("res_sb", [P, D], F32)
         nc.sync.dma_start(res_sb[:], res)
         neg_max = tile("neg_max", [P, 1], F32, "scores")
         nc.vector.tensor_reduce(out=neg_max[:], in_=means[:, 0:SPANS], axis=AX.X, op=ALU.max, negate=True)
@@ -221,7 +220,7 @@ def tile_attend_hvspanread_q_kernel(tc, query, keys_words, keys_scales, gout, va
         key_rows(0)
         key_rows(2)
 
-        zz = tile("zz", [P, 2 * SPANS], F32, "dq_raw")
+        zz = tile("zz", [P, 2 * SPANS], F32, "plane2")
         total = tile("total", [P, 1], F32)
         nc.vector.scalar_tensor_tensor(out=zz[:], in0=sums[:], scalar=1.0, in1=shares[:],
                                        op0=ALU.mult, op1=ALU.mult, accum_out=total[:])
@@ -249,7 +248,7 @@ def tile_attend_hvspanread_q_kernel(tc, query, keys_words, keys_scales, gout, va
         for n, src in enumerate(sources):
             nc.tensor.matmul(gs_ps[:, n % PACK, :], lhsT=src, rhs=ident[:], is_transpose=True,
                              start=(n == 0), stop=(n == len(sources) - 1))
-        gs_bf = tile("gs_bf", [P, P, PACK], BF16, "go_raw")
+        gs_bf = tile("gs_bf", [P, P, PACK], BF16, "plane3")
         nc.vector.scalar_tensor_tensor(out=gs_bf[:], in0=gs_ps[:].rearrange("p t q -> p q t"), scalar=-0.5,
                                        in1=fs_pt[:].rearrange("p (o t) -> p o t", o=1).to_broadcast([P, P, PACK]),
                                        op0=ALU.mult, op1=ALU.mult)

from contextlib import ExitStack

import concourse.mybir as mybir
from concourse.masks import make_identity

F32 = mybir.dt.float32
BF16 = mybir.dt.bfloat16
I32 = mybir.dt.int32
U32 = mybir.dt.uint32
U16 = mybir.dt.uint16
U8 = mybir.dt.uint8
FP8X4 = mybir.dt.float8_e4m3fn_x4
FP4X4 = mybir.dt.float4_e2m1fn_x4
ALU = mybir.AluOpType
ACT = mybir.ActivationFunctionType
AX = mybir.AxisListType

P = 128
POOL = 2048
SLOTS = 512
SPANS = 64
SPAN = 8
PACK = 4
D = 512
SCALAR_PLANES = 2
FLOPS = 4 * 2 * 128 * 512 * 512


def tile_attend_hvspanread_q_kernel(tc, query, keys_words, keys_scales, gout, vals_words, vals_scales,
                                     size, dquery, fs, keyrows, res, offs, out):
    nc = tc.nc
    with ExitStack() as ctx:
        sb = ctx.enter_context(tc.tile_pool(name="sb", bufs=1))
        ps = ctx.enter_context(tc.psum_pool(name="ps", bufs=1))

        def tile(name, shape, dtype, tag=None):
            return sb.tile(shape, dtype, name=name, tag=tag or name, align_bytes=64)

        offsets = sb.tile([P, SLOTS // 16], U16, name="offsets")
        nc.sync.dma_start(offsets[:], offs)

        def load_words(name, words):
            t = tile(name, [P, POOL], U16)
            nc.sync.dma_start(t[:].bitcast(I32), words[0].bitcast(I32))
            return t

        def load_scales(name, scales, clear):
            t = tile(name, [P, POOL], U8)
            clear.memset(t[:].bitcast(I32), 0)
            for r in range(4):
                nc.sync.dma_start(t[r:P:32, :].bitcast(I32), scales[0, r:16:4, :].bitcast(I32))
            return t

        def load_rows(name, rows):
            t = tile(name, [P, PACK, P], F32)
            nc.sync.dma_start(t[:], rows.rearrange("(p t) q -> p t q", t=PACK))
            return t

        def load_by_slot(name, row, queue, tag=None):
            t = tile(name, [P, PACK], F32, tag)
            queue.dma_start(t[:], row.rearrange("o (p t) -> (o p) t", t=PACK))
            return t

        k_words = load_words("k_words", keys_words)
        k_scales = load_scales("k_scales", keys_scales, nc.gpsimd)
        q_raw = load_rows("q_raw", query)
        dq_raw = load_rows("dq_raw", dquery)
        v_scales = load_scales("v_scales", vals_scales, nc.vector)
        ident = tile("ident", [P, P], F32)
        make_identity(nc, ident[:])
        go_raw = load_rows("go_raw", gout)
        size_pt = load_by_slot("size_pt", size, nc.sync)
        v_words = load_words("v_words", vals_words)

        def gather(name, window, dtype, tag=None):
            t = tile(name, [P, SLOTS], dtype, tag)
            nc.vector.tensor_copy(t[:], window[:].indirect(offsets[:]))
            return t

        def interleave(dst, raw):
            nc.scalar.copy(out=dst.rearrange("p (c i t) -> p c t i", i=4, t=PACK),
                           in_=raw[:].rearrange("p t (c i) -> p c t i", i=4))

        kw_g = gather("kw_g", k_words, U16)
        ks_g = gather("ks_g", k_scales, U8)
        qd_bf = tile("qd_bf", [P, 2 * PACK * P], BF16)
        interleave(qd_bf[:, 0:PACK * P], q_raw)
        interleave(qd_bf[:, PACK * P:2 * PACK * P], dq_raw)
        qd_codes = tile("qd_codes", [P, 2 * P], U32)
        qd_scales = tile("qd_scales", [P, 2 * P], U8)
        nc.vector.quantize_mx(out=qd_codes[:].bitcast(FP8X4), scales=qd_scales[:], in_=qd_bf[:])
        a_ps = ps.tile([P, SLOTS], F32, name="a_ps", tag="a_gq")
        ta_ps = ps.tile([P, SLOTS], F32, name="ta_ps", tag="ta")
        for half, bank in enumerate((a_ps, ta_ps)):
            cols = slice(half * P, (half + 1) * P)
            nc.tensor.matmul_mx(out=bank[:], lhsT=qd_codes[:, cols].bitcast(FP8X4), lhsT_scale=qd_scales[:, cols],
                                rhs=kw_g[:].bitcast(FP4X4), rhs_scale=ks_g[:], start=True, stop=True)

        def by_place(bank):
            return bank[:].rearrange("q (g j) -> q j g", j=SPAN)

        th = tile("th", [P, SPAN, SPANS], F32)
        nc.scalar.activation(out=th[:], in_=by_place(a_ps), func=ACT.Tanh, scale=0.5)
        scores = tile("scores", [P, SPAN, 2 * SPANS], F32)
        nc.scalar.copy(out=scores[:, :, 0:SPANS], in_=by_place(a_ps))
        nc.scalar.copy(out=scores[:, :, SPANS:2 * SPANS], in_=by_place(ta_ps))

        size_ps = ps.tile([P, PACK, P], F32, name="size_ps", tag="size_gs")
        for t in range(PACK):
            nc.tensor.transpose(size_ps[:, t, :], size_pt[:, t:t + 1].to_broadcast([P, P]), ident[:])
        half_size = tile("half_size", [P, SPAN, SPANS], F32)
        nc.scalar.activation(out=half_size[:].rearrange("q (h t) g -> q h t g", h=2),
                             in_=size_ps[:].rearrange("q t (g h) -> q h t g", h=2), func=ACT.Copy, scale=0.5)

        vs_g = gather("vs_g", v_scales, U8, "qd_bf")
        go_bf = tile("go_bf", [P, PACK * P], BF16)
        interleave(go_bf[:], go_raw)
        go_codes = tile("go_codes", [P, P], U32)
        go_scales = tile("go_scales", [P, P], U8)
        nc.vector.quantize_mx(out=go_codes[:].bitcast(FP8X4), scales=go_scales[:], in_=go_bf[:])
        vw_g = tile("vw_g", [P, SLOTS], U16)
        c0_halves = []
        for half in range(2):
            cols = slice(half * SLOTS // 2, (half + 1) * SLOTS // 2)
            nc.vector.tensor_copy(vw_g[:, cols], v_words[:].indirect(offsets[:, half * 16:(half + 1) * 16]))
            bank = ps.tile([P, SLOTS // 2], F32, name="c0_%d" % half, tag="c0_%d" % half)
            nc.tensor.matmul_mx(out=bank[:], lhsT=go_codes[:].bitcast(FP8X4), lhsT_scale=go_scales[:],
                                rhs=vw_g[:, cols].bitcast(FP4X4), rhs_scale=vs_g[:, cols], start=True, stop=True)
            c0_halves.append(bank)

        planes = []
        for b in range(D // P):
            t = tile("plane%d" % b, [P, POOL], F32)
            nc.sync.dma_start(t[:], keyrows[b * P:(b + 1) * P, :])
            planes.append(t)
        fs_pt = load_by_slot("fs_pt", fs, nc.sync)

        kt_bf = [tile("kt_bf%d" % half, [P, D // 2 * PACK], BF16) for half in range(2)]


        def key_rows(b):
            if b < SCALAR_PLANES:
                narrow = tile("narrow%d" % b, [P, POOL], BF16, (None, "grads")[b])
                for c in range(0, POOL, 512):
                    nc.scalar.activation(out=narrow[:, c:c + 512], in_=planes[b][:, c:c + 512], func=ACT.Copy)
                rows = tile("rows%d" % b, [P, SLOTS], BF16, ("scores", "w_n")[b])
                nc.scalar.activation(out=rows[:], in_=narrow[:].indirect(offsets[:]), func=ACT.Copy)
            else:
                rows = gather("rows%d" % b, planes[b], BF16, ("a_n", "u1")[b - SCALAR_PLANES])
            words = rows[:].bitcast(F32)
            xt = ps.tile([P, 2, P], F32, name="xt%d" % b, tag=("c0_0", "means", "c0_1", "turned")[b])
            for u in range(2):
                nc.tensor.transpose(xt[:, u, :], words[:, u:SLOTS // 2:2], ident[:])
            block = kt_bf[b // 2][:, (b % 2) * P * PACK:(b % 2 + 1) * P * PACK]
            nc.scalar.copy(out=block.bitcast(F32).rearrange("p (d u) -> p d u", u=2),
                           in_=xt[:].rearrange("p u d -> p d u"))

        def span_sums(name, src, factor):
            turned = ps.tile([P, P], F32, name=name + "_t", tag="turned")
            for j in range(SPAN):
                nc.tensor.matmul(turned[:], lhsT=src[:, j, :], rhs=ident[:], is_transpose=True,
                                 start=(j == 0), stop=(j == SPAN - 1))
            staged = tile(name + "_s", [P, P], F32)
            nc.scalar.activation(out=staged[:], in_=turned[:], func=ACT.Copy, scale=factor)
            back = ps.tile([P, P], F32, name=name, tag=name)
            nc.tensor.transpose(back[:], staged[:], ident[:])
            return back

        means = span_sums("means", scores, 1.0 / SPAN)

        cs = tile("cs", [P, SPAN, SPANS], F32)
        grads = tile("grads", [P, SPAN, 2 * SPANS], F32)
        drr = grads[:, :, 0:SPANS]
        tdrr = grads[:, :, SPANS:2 * SPANS]
        ta = scores[:, :, SPANS:2 * SPANS]
        a_n = tile("a_n", [P, SPAN, SPANS], F32)
        b_2 = tile("b_2", [P, SPAN, SPANS], F32)
        halves = [slice(0, SPANS // 2), slice(SPANS // 2, SPANS)]
        for s, bank in zip(halves, c0_halves):
            nc.vector.tensor_tensor(out=cs[:, :, s], in0=by_place(bank), in1=half_size[:, :, s], op=ALU.mult)
        for dst, in0, scalar, op0, in1 in ((drr, th, 1.0, ALU.add, cs), (a_n, th, 1.0, ALU.subtract, drr),
                                           (tdrr, a_n, -0.5, ALU.mult, ta)):
            for s in halves:
                nc.vector.scalar_tensor_tensor(out=dst[:, :, s], in0=in0[:, :, s], scalar=scalar, in1=in1[:, :, s],
                                               op0=op0, op1=ALU.mult)
        res_sb = tile("res_sb", [P, D], F32)
        nc.sync.dma_start(res_sb[:], res)
        neg_max = tile("neg_max", [P, 1], F32, "scores")
        nc.vector.tensor_reduce(out=neg_max[:], in_=means[:, 0:SPANS], axis=AX.X, op=ALU.max, negate=True)
        p_sb = tile("p_sb", [P, SPANS], F32)
        z = tile("z", [P, 1], F32)
        nc.scalar.activation(out=p_sb[:], in_=means[:, 0:SPANS], func=ACT.Exp, bias=neg_max[:], accum_out=z[:])
        sums = span_sums("sums", grads, 0.25)

        nc.vector.scalar_tensor_tensor(out=b_2[:], in0=th[:], scalar=2.0, in1=tdrr, op0=ALU.mult, op1=ALU.mult)
        rz = tile("rz", [P, 1], F32)
        nc.vector.reciprocal(out=rz[:], in_=z[:])
        shares = tile("shares", [P, 2 * SPANS], F32)
        tr = shares[:, 0:SPANS]
        r = shares[:, SPANS:2 * SPANS]
        mu = tile("mu", [P, 1], F32)
        r_ts = tile("r_ts", [P, SPANS], F32)
        nc.vector.scalar_tensor_tensor(out=r_ts[:], in0=p_sb[:], scalar=rz[:], in1=means[:, SPANS:2 * SPANS],
                                       op0=ALU.mult, op1=ALU.mult, accum_out=mu[:])
        nc.vector.tensor_scalar(out=r, in0=p_sb[:], scalar1=rz[:], scalar2=None, op0=ALU.mult)
        nc.vector.scalar_tensor_tensor(out=tr, in0=means[:, SPANS:2 * SPANS], scalar=mu[:], in1=r,
                                       op0=ALU.subtract, op1=ALU.mult)

        def spread(x, places):
            return x.rearrange("q (a g b) -> q a g b", a=1, b=1).to_broadcast([P, places, SPANS, 2])

        terms = []
        for name, slotwise, spanwise in (("term_b", b_2, r), ("term_a", a_n, tr)):
            t = tile(name, [P, PACK, P], F32)
            nc.vector.tensor_tensor(out=t[:].rearrange("q t (g h) -> q t g h", h=2),
                                    in0=slotwise[:].rearrange("q (h t) g -> q t g h", h=2),
                                    in1=spread(spanwise, PACK), op=ALU.mult)
            terms.append(t)

        key_rows(0)
        key_rows(2)

        zz = tile("zz", [P, 2 * SPANS], F32, "plane2")
        total = tile("total", [P, 1], F32)
        nc.vector.scalar_tensor_tensor(out=zz[:], in0=sums[:], scalar=1.0, in1=shares[:],
                                       op0=ALU.mult, op1=ALU.mult, accum_out=total[:])
        r_dr = tile("r_dr", [P, SPANS], F32)
        m = tile("m", [P, 1], F32)
        nc.vector.scalar_tensor_tensor(out=r_dr[:], in0=sums[:, 0:SPANS], scalar=1.0, in1=r,
                                       op0=ALU.mult, op1=ALU.mult, accum_out=m[:])
        u1 = tile("u1", [P, SPANS], F32)
        u2 = tile("u2", [P, SPANS], F32)
        nc.vector.scalar_tensor_tensor(out=u2[:], in0=r, scalar=total[:], in1=zz[:, SPANS:2 * SPANS],
                                       op0=ALU.mult, op1=ALU.subtract)
        nc.vector.scalar_tensor_tensor(out=u1[:], in0=tr, scalar=m[:], in1=zz[:, 0:SPANS],
                                       op0=ALU.mult, op1=ALU.subtract)
        w_n = tile("w_n", [P, P], F32)

        def twice(x):
            return x[:].rearrange("q (g b) -> q g b", b=1).to_broadcast([P, SPANS, 2])

        nc.vector.tensor_tensor(out=w_n[:].rearrange("q (g h) -> q g h", h=2), in0=twice(u1), in1=twice(u2), op=ALU.add)

        key_rows(3)

        gs_ps = ps.tile([P, PACK, P], F32, name="gs_ps", tag="size_gs")
        sources = [terms[0][:, t, :] for t in range(PACK)] + [terms[1][:, t, :] for t in range(PACK)] + [w_n[:]] * PACK
        for n, src in enumerate(sources):
            nc.tensor.matmul(gs_ps[:, n % PACK, :], lhsT=src, rhs=ident[:], is_transpose=True,
                             start=(n == 0), stop=(n == len(sources) - 1))
        gs_bf = tile("gs_bf", [P, P, PACK], BF16, "plane3")
        nc.vector.scalar_tensor_tensor(out=gs_bf[:], in0=gs_ps[:].rearrange("p t q -> p q t"), scalar=-0.5,
                                       in1=fs_pt[:].rearrange("p (o t) -> p o t", o=1).to_broadcast([P, P, PACK]),
                                       op0=ALU.mult, op1=ALU.mult)
        key_rows(1)
        gs_codes = tile("gs_codes", [P, P], U32)
        gs_scales = tile("gs_scales", [P, P], U8)
        nc.vector.quantize_mx(out=gs_codes[:].bitcast(FP8X4), scales=gs_scales[:],
                              in_=gs_bf[:].rearrange("p q t -> p (q t)"))
        y = tile("y", [P, D], F32)
        for half, tag in ((1, "a_gq"), (0, "ta")):
            cols = slice(half * D // 2, (half + 1) * D // 2)
            kt_codes = tile("kt_codes%d" % half, [P, D // 2], U32, ("u1", None)[half])
            kt_scales = tile("kt_scales%d" % half, [P, D // 2], U8)
            nc.vector.quantize_mx(out=kt_codes[:].bitcast(FP8X4), scales=kt_scales[:], in_=kt_bf[half][:])
            gq_ps = ps.tile([P, D // 2], F32, name="gq%d" % half, tag=tag)
            nc.tensor.matmul_mx(out=gq_ps[:], lhsT=gs_codes[:].bitcast(FP8X4), lhsT_scale=gs_scales[:],
                                rhs=kt_codes[:].bitcast(FP8X4), rhs_scale=kt_scales[:],
                                start=True, stop=True)
            nc.vector.tensor_tensor(out=y[:, cols], in0=gq_ps[:], in1=res_sb[:, cols], op=ALU.add)
            nc.sync.dma_start(out[:, cols], y[:, cols])
